import numpy as np
import ml_dtypes


def mxq(x, axis, fmt="e4m3"):
    dtype, down = {"e4m3": (ml_dtypes.float8_e4m3fn, 7), "e5m2": (ml_dtypes.float8_e5m2, 14)}[fmt]
    v = np.moveaxis(np.asarray(x, np.float32).astype(ml_dtypes.bfloat16).astype(np.float64), axis, -1)
    blocks = v.reshape(v.shape[:-1] + (-1, 32))
    amax = np.abs(blocks).max(-1, keepdims=True)
    byte = np.maximum(np.where(amax > 0, np.frexp(amax)[1] - 1 + 127, 0) - down, 1)
    scale = np.exp2(byte - 127.0)
    codes = (blocks / scale).astype(np.float32).astype(dtype).astype(np.float64)
    return np.moveaxis((codes * scale).reshape(v.shape), -1, axis)


WIDE = False


def mx_kscale(k):
    if not WIDE:
        return np.ones(k)
    levels = np.array([10, -10, 5, -5, 0])
    if k % 512:
        return np.exp2(np.random.permutation(np.resize(levels, k // 32))).repeat(32)
    a = np.empty((k // 512, 16))
    for p in range(k // 512):
        a[p, :8] = np.random.permutation(np.resize(levels, 8))
        for g in range(8):
            far = levels[np.abs(levels - a[p, g]) >= 10]
            a[p, g + 8] = far[np.random.randint(len(far))]
    return np.exp2(a.ravel()).repeat(32)


def f64(x):
    return np.asarray(x).astype(np.float64)


def striped(idx):
    return np.tile(idx.reshape(-1, 16).T, (8, 1)).astype(np.uint16)


def unstriped(offs):
    return offs[:16].T.reshape(-1).astype(np.int64)


def relu2(v):
    return np.maximum(v, 0.0) ** 2


K, T, D, S, V, H, N = 1536, 1024, 3, 512, 256, 1024, 128


def setup_inputs():
    n = np.random.standard_normal
    s = mx_kscale(K)[:, None]
    u = mx_kscale(H)
    return {
        "xT": (n((K, T)) * s).astype(np.float32),
        "w1": (n((K, H)) / np.sqrt(K) / s * u).astype(np.float32),
        "w2": (n((H, N)) / np.sqrt(H) / u[:, None] ** 2).astype(np.float32),
        "gate": np.tile(np.random.uniform(0.2, 1.0, (D, 1, V)) / np.sqrt(D), (1, N, 1)).astype(np.float32),
        "offs": striped(np.random.permutation(T)[:S]),
        "pos1": striped(np.random.permutation(S)[:V]),
        "pos2": striped(np.random.permutation(S)[:V]),
        "pos3": striped(np.random.permutation(S)[:V]),
    }


def reference(xT, w1, w2, gate, offs, pos1, pos2, pos3):
    idx = unstriped(offs)
    xq = mxq(f64(xT)[:, idx], 0, "e4m3")
    h = relu2(mxq(f64(w1), 0, "e4m3").T @ xq)
    y = mxq(f64(w2), 0, "e4m3").T @ mxq(h, 0, "e4m3")
    return sum(f64(gate[d]) * y[:, unstriped(p)] for d, p in enumerate((pos1, pos2, pos3)))

@@ -1,0 +1,211 @@
+from contextlib import ExitStack
+
+import concourse.mybir as mybir
+
+K, T, S, H, N, D, V = 1536, 1024, 512, 1024, 128, 3, 256
+FLOPS = 2 * S * (K * H + H * N)
+
+F32 = mybir.dt.float32
+BF16 = mybir.dt.bfloat16
+U32 = mybir.dt.uint32
+U16 = mybir.dt.uint16
+U8 = mybir.dt.uint8
+FP8X4 = mybir.dt.float8_e4m3fn_x4
+ACT = mybir.ActivationFunctionType
+ALU = mybir.AluOpType
+
+P = 128
+PACK = 4
+K_PASS = P * PACK
+PASSES = K // K_PASS
+HALVES = H // K_PASS
+W = 512
+
+X_SCALAR = 400
+W1_SCALAR = (80, 64)
+W1_SCALAR_LAST = 48
+
+
+def tile_picked_sub_mlp_relu2_sub_e_kernel(tc, xT, w1, w2, gate, offs, pos1, pos2, pos3, out):
+    nc = tc.nc
+    with ExitStack() as ctx:
+        keep = ctx.enter_context(tc.tile_pool(name="keep", bufs=1))
+        psum = ctx.enter_context(tc.psum_pool(name="psum", bufs=1))
+
+        offs_t = keep.tile([P, S // 16], U16, name="offs_t")
+        pos_t = [keep.tile([P, V // 16], U16, name=f"pos{d}_t") for d in range(D)]
+
+        x_scales = keep.tile([P, T], U8, name="x_scales", align_bytes=64)
+        nc.gpsimd.memset(x_scales[:], 0)
+
+        w2_raw = keep.tile([P, HALVES, PACK, N], F32, name="w2_raw")
+        nc.sync.dma_start(out=w2_raw[:], in_=w2.rearrange("(g p j) m -> p g j m", p=P, j=PACK))
+        x_raw = {}
+        for s in range(PASSES):
+            for c in range(T // W):
+                raw = keep.tile([P, PACK, W], F32, name=f"x_raw{s}{c}")
+                nc.sync.dma_start(
+                    out=raw[:],
+                    in_=xT[s * K_PASS : (s + 1) * K_PASS, c * W : (c + 1) * W].rearrange("(p j) w -> p j w", j=PACK),
+                )
+                x_raw[s, c] = raw
+            if s == 0:
+                nc.sync.dma_start(offs_t[:], offs)
+        w1_raw = {}
+        for h in range(HALVES):
+            for s in range(PASSES):
+                pieces = 2 if h == HALVES - 1 and s == PASSES - 1 else 1
+                width = W // pieces
+                w1_raw[h, s] = []
+                for c in range(pieces):
+                    raw = keep.tile([P, PACK, width], F32, name=f"w1_raw{h}{s}{c}")
+                    first = h * W + c * width
+                    nc.sync.dma_start(
+                        out=raw[:],
+                        in_=w1[s * K_PASS : (s + 1) * K_PASS, first : first + width].rearrange("(p j) w -> p j w", j=PACK),
+                    )
+                    w1_raw[h, s].append(raw)
+            if h == 0:
+                for d, pos in enumerate((pos1, pos2, pos3)):
+                    nc.sync.dma_start(pos_t[d][:], pos)
+        gate_t = keep.tile([P, D, V], F32, name="gate_t")
+        nc.sync.dma_start(out=gate_t[:], in_=gate.rearrange("d m v -> m d v"))
+
+        w2_codes = keep.tile([P, HALVES, N], U32, name="w2_codes", align_bytes=64)
+        w2_scales = keep.tile([P, HALVES, N], U8, name="w2_scales", align_bytes=64)
+        w2_grouped = keep.tile([P, HALVES, N * PACK], BF16, name="w2_grouped", align_bytes=64)
+        for g in range(HALVES):
+            nc.scalar.copy(
+                w2_grouped[:, g, :].rearrange("p (c i j) -> p c j i", i=4, j=PACK),
+                w2_raw[:, g].rearrange("p j (c i) -> p c j i", i=4),
+            )
+        nc.vector.quantize_mx(
+            out=w2_codes[:].rearrange("p g m -> p (g m)").bitcast(FP8X4),
+            scales=w2_scales[:].rearrange("p g m -> p (g m)"),
+            in_=w2_grouped[:].rearrange("p g m -> p (g m)"),
+        )
+
+        x_words, g_words = [], []
+        for s in range(PASSES):
+            words = keep.tile([P, T], U32, name=f"x_words{s}", align_bytes=64)
+            x_words.append(words)
+            grouped = keep.tile([P, T * PACK], BF16, name=f"x_grouped{s}", align_bytes=64)
+            for c in range(T // W):
+                raw = x_raw[s, c]
+                src = raw[:].rearrange("p j (c i) -> p c j i", i=4)
+                dst = grouped[:, c * W * PACK : (c + 1) * W * PACK].rearrange("p (c i j) -> p c j i", i=4, j=PACK)
+                cut = X_SCALAR // 4
+                nc.scalar.copy(dst[:, :cut], src[:, :cut])
+                nc.vector.tensor_copy(out=dst[:, cut:], in_=src[:, cut:])
+                nc.vector.quantize_mx(
+                    out=words[:, c * W : (c + 1) * W].bitcast(FP8X4),
+                    scales=x_scales[4 * s : P, c * W : (c + 1) * W],
+                    in_=grouped[:, c * W * PACK : (c + 1) * W * PACK],
+                )
+            picked = keep.tile([P, S], U32, name=f"g_words{s}", align_bytes=64)
+            nc.vector.tensor_copy(picked[:], words[:].indirect(offs_t[:]))
+            g_words.append(picked)
+        g_scales = keep.tile([P, S], U8, name="g_scales", align_bytes=64)
+        nc.vector.tensor_copy(g_scales[:], x_scales[:].indirect(offs_t[:]))
+
+        h_codes, h_scales = [], []
+        HALF = S // 2
+        for h in range(HALVES):
+            if h == 0:
+                banks = {(t, 0): psum.tile([P, S], F32, name=f"bank{t}", tag=f"b{t}") for t in range(PACK)}
+                blocks = [slice(0, S)]
+            else:
+                banks = {
+                    (t, b): psum.tile([P, HALF], F32, name=f"bank1{t}{b}", tag=f"b{4 * (1 - b) + t}")
+                    for b in range(2)
+                    for t in range(PACK)
+                }
+                blocks = [slice(0, HALF), slice(HALF, S)]
+            for s in range(PASSES):
+                last = h == HALVES - 1 and s == PASSES - 1
+                grouped = keep.tile([P, W * PACK], BF16, name=f"w1_grouped{h}{s}", align_bytes=64)
+                m0 = 0
+                for raw in w1_raw[h, s]:
+                    src = raw[:].rearrange("p j (m t) -> p m j t", t=PACK)
+                    m = P // len(w1_raw[h, s])
+                    dst = grouped[:].rearrange("p (t m j) -> p m j t", t=PACK, j=PACK)[:, m0 : m0 + m]
+                    m0 += m
+                    cut = (W1_SCALAR_LAST if last else W1_SCALAR[h]) * m // P
+                    nc.scalar.copy(dst[:, :cut], src[:, :cut])
+                    nc.vector.tensor_copy(out=dst[:, cut:], in_=src[:, cut:])
+                codes = keep.tile([P, W], U32, name=f"w1_codes{h}{s}", align_bytes=64)
+                scales = keep.tile([P, W], U8, name=f"w1_scales{h}{s}", align_bytes=64)
+                step = 2 * P if last else W
+                for q in range(0, W, step):
+                    nc.vector.quantize_mx(
+                        out=codes[:, q : q + step].bitcast(FP8X4),
+                        scales=scales[:, q : q + step],
+                        in_=grouped[:, PACK * q : PACK * (q + step)],
+                    )
+                for b, cols in enumerate(blocks):
+                    for t in range(PACK):
+                        nc.tensor.matmul_mx(
+                            out=banks[t, b][:],
+                            lhsT=codes[:, t * P : (t + 1) * P].bitcast(FP8X4),
+                            lhsT_scale=scales[:, t * P : (t + 1) * P],
+                            rhs=g_words[s][:, cols].bitcast(FP8X4),
+                            rhs_scale=g_scales[4 * s : P, cols],
+                            start=(s == 0),
+                            stop=(s == PASSES - 1),
+                        )
+            r = keep.tile([P, PACK, S], F32, name=f"r{h}")
+            for b, cols in enumerate(blocks):
+                for t in range(PACK):
+                    if t % 2 == 0:
+                        nc.scalar.activation(r[:, t, cols], banks[t, b][:], ACT.Relu)
+                    else:
+                        nc.vector.tensor_scalar_max(r[:, t, cols], banks[t, b][:], 0.0)
+            h_grouped = keep.tile([P, S * PACK], BF16, name=f"h_grouped{h}", align_bytes=64)
+            codes = keep.tile([P, S], U32, name=f"h_codes{h}", align_bytes=64)
+            scales = keep.tile([P, S], U8, name=f"h_scales{h}", align_bytes=64)
+            for b in range(2):
+                src = r[:, :, b * HALF : (b + 1) * HALF].rearrange("p t (c i) -> p c t i", i=4)
+                dst = h_grouped[:, b * HALF * PACK : (b + 1) * HALF * PACK].rearrange("p (c i t) -> p c t i", i=4, t=PACK)
+                if b == 1:
+                    nc.scalar.activation(dst, src, ACT.Square)
+                else:
+                    nc.vector.tensor_tensor(dst, src, src, ALU.mult)
+            for b in range(2):
+                nc.vector.quantize_mx(
+                    out=codes[:, b * HALF : (b + 1) * HALF].bitcast(FP8X4),
+                    scales=scales[:, b * HALF : (b + 1) * HALF],
+                    in_=h_grouped[:, b * HALF * PACK : (b + 1) * HALF * PACK],
+                )
+            h_codes.append(codes)
+            h_scales.append(scales)
+
+        y_banks = [psum.tile([P, HALF], F32, name=f"y_bank{b}", tag=f"b{4 + b}") for b in range(2)]
+        for b in range(2):
+            cols = slice(b * HALF, (b + 1) * HALF)
+            for h in range(HALVES):
+                nc.tensor.matmul_mx(
+                    out=y_banks[b][:],
+                    lhsT=w2_codes[:, h, :].bitcast(FP8X4),
+                    lhsT_scale=w2_scales[:, h, :],
+                    rhs=h_codes[h][:, cols].bitcast(FP8X4),
+                    rhs_scale=h_scales[h][:, cols],
+                    start=(h == 0),
+                    stop=(h == HALVES - 1),
+                )
+
+        y = keep.tile([P, S], F32, name="y")
+        nc.scalar.copy(y[:, : S // 2], y_banks[0][:])
+        nc.vector.tensor_copy(out=y[:, S // 2 :], in_=y_banks[1][:])
+        prods = []
+        for d in range(D):
+            prod = keep.tile([P, V], F32, name=f"prod{d}")
+            nc.vector.tensor_tensor(prod[:], y[:].indirect(pos_t[d][:]), gate_t[:, d, :], ALU.mult)
+            prods.append(prod)
+        pair = keep.tile([P, V], F32, name="pair")
+        result = keep.tile([P, V], F32, name="result")
+        halves = [slice(0, V // 2), slice(V // 2, V)]
+        for cols in halves:
+            nc.vector.tensor_tensor(pair[:, cols], prods[0][:, cols], prods[1][:, cols], ALU.add)
+        for cols in halves:
+            nc.vector.tensor_tensor(result[:, cols], pair[:, cols], prods[2][:, cols], ALU.add)
+            (nc.sync if cols.start == 0 else nc.scalar).dma_start(out=out[:, cols], in_=result[:, cols])

@@ -20,10 +20,13 @@ K_PASS = P * PACK
 PASSES = K // K_PASS
 HALVES = H // K_PASS
 W = 512
+HALF = S // 2
 
-X_SCALAR = 400
-W1_SCALAR = (80, 64)
-W1_SCALAR_LAST = 48
+X_SCALAR = 320
+W1_SCALAR = ((80, 80, 80), (32, 32, 48))
+RELU0 = (True, False, True, True)
+RELU1 = ((True, False, True, False), (True, False, True, True))
+SQUARE = ((True, True, True, False), (False, True, False, True))
 
 
 def tile_picked_sub_mlp_relu2_sub_e_kernel(tc, xT, w1, w2, gate, offs, pos1, pos2, pos3, out):
@@ -32,120 +35,106 @@ def tile_picked_sub_mlp_relu2_sub_e_kernel(tc, xT, w1, w2, gate, offs, pos1, pos
         keep = ctx.enter_context(tc.tile_pool(name="keep", bufs=1))
         psum = ctx.enter_context(tc.psum_pool(name="psum", bufs=1))
 
+        def copy(on_scalar, dst, src):
+            if on_scalar:
+                nc.scalar.copy(dst, src)
+            else:
+                nc.vector.tensor_copy(out=dst, in_=src)
+
+        def quantize(codes, scales, grouped, cols, plane=0):
+            nc.vector.quantize_mx(
+                out=codes[:, cols].bitcast(FP8X4),
+                scales=scales[plane:P, cols],
+                in_=grouped[:, PACK * cols.start : PACK * cols.stop],
+            )
+
+        def operand(name, width):
+            return (
+                keep.tile([P, width * PACK], BF16, name=f"{name}_grouped", align_bytes=64),
+                keep.tile([P, width], U32, name=f"{name}_codes", align_bytes=64),
+                keep.tile([P, width], U8, name=f"{name}_scales", align_bytes=64),
+            )
+
         offs_t = keep.tile([P, S // 16], U16, name="offs_t")
         pos_t = [keep.tile([P, V // 16], U16, name=f"pos{d}_t") for d in range(D)]
-
+        w2_raw = keep.tile([P, HALVES, PACK, N], F32, name="w2_raw")
         x_scales = keep.tile([P, T], U8, name="x_scales", align_bytes=64)
         nc.gpsimd.memset(x_scales[:], 0)
 
-        w2_raw = keep.tile([P, HALVES, PACK, N], F32, name="w2_raw")
-        nc.sync.dma_start(out=w2_raw[:], in_=w2.rearrange("(g p j) m -> p g j m", p=P, j=PACK))
-        x_raw = {}
+        def load_rows(name, source, s, first, width):
+            raw = keep.tile([P, PACK, width], F32, name=name)
+            rows = source[s * K_PASS : (s + 1) * K_PASS, first : first + width]
+            nc.sync.dma_start(out=raw[:], in_=rows.rearrange("(p j) w -> p j w", j=PACK))
+            return raw
+
+        def load_w2():
+            nc.sync.dma_start(out=w2_raw[:], in_=w2.rearrange("(g p j) m -> p g j m", p=P, j=PACK))
+
+        x_raw, w1_raw = {}, {}
         for s in range(PASSES):
             for c in range(T // W):
-                raw = keep.tile([P, PACK, W], F32, name=f"x_raw{s}{c}")
-                nc.sync.dma_start(
-                    out=raw[:],
-                    in_=xT[s * K_PASS : (s + 1) * K_PASS, c * W : (c + 1) * W].rearrange("(p j) w -> p j w", j=PACK),
-                )
-                x_raw[s, c] = raw
+                x_raw[s, c] = load_rows(f"x_raw{s}{c}", xT, s, c * W, W)
             if s == 0:
                 nc.sync.dma_start(offs_t[:], offs)
-        w1_raw = {}
         for h in range(HALVES):
             for s in range(PASSES):
-                pieces = 2 if h == HALVES - 1 and s == PASSES - 1 else 1
-                width = W // pieces
-                w1_raw[h, s] = []
-                for c in range(pieces):
-                    raw = keep.tile([P, PACK, width], F32, name=f"w1_raw{h}{s}{c}")
-                    first = h * W + c * width
-                    nc.sync.dma_start(
-                        out=raw[:],
-                        in_=w1[s * K_PASS : (s + 1) * K_PASS, first : first + width].rearrange("(p j) w -> p j w", j=PACK),
-                    )
-                    w1_raw[h, s].append(raw)
+                pieces = 2 if h == 1 and s == PASSES - 1 else 1
+                w1_raw[h, s] = [
+                    load_rows(f"w1_raw{h}{s}{c}", w1, s, h * W + c * (W // pieces), W // pieces) for c in range(pieces)
+                ]
             if h == 0:
                 for d, pos in enumerate((pos1, pos2, pos3)):
                     nc.sync.dma_start(pos_t[d][:], pos)
+        load_w2()
         gate_t = keep.tile([P, D, V], F32, name="gate_t")
         nc.sync.dma_start(out=gate_t[:], in_=gate.rearrange("d m v -> m d v"))
 
-        w2_codes = keep.tile([P, HALVES, N], U32, name="w2_codes", align_bytes=64)
-        w2_scales = keep.tile([P, HALVES, N], U8, name="w2_scales", align_bytes=64)
-        w2_grouped = keep.tile([P, HALVES, N * PACK], BF16, name="w2_grouped", align_bytes=64)
-        for g in range(HALVES):
-            nc.scalar.copy(
-                w2_grouped[:, g, :].rearrange("p (c i j) -> p c j i", i=4, j=PACK),
-                w2_raw[:, g].rearrange("p j (c i) -> p c j i", i=4),
-            )
-        nc.vector.quantize_mx(
-            out=w2_codes[:].rearrange("p g m -> p (g m)").bitcast(FP8X4),
-            scales=w2_scales[:].rearrange("p g m -> p (g m)"),
-            in_=w2_grouped[:].rearrange("p g m -> p (g m)"),
-        )
+        w2_grouped, w2_codes, w2_scales = operand("w2", HALVES * N)
 
-        x_words, g_words = [], []
+        def prepare_w2():
+            for g in range(HALVES):
+                nc.vector.tensor_copy(
+                    out=w2_grouped[:, g * N * PACK : (g + 1) * N * PACK].rearrange("p (c i j) -> p c j i", i=4, j=PACK),
+                    in_=w2_raw[:, g].rearrange("p j (c i) -> p c j i", i=4),
+                )
+            quantize(w2_codes, w2_scales, w2_grouped, slice(0, HALVES * N))
+
+        g_words = []
         for s in range(PASSES):
             words = keep.tile([P, T], U32, name=f"x_words{s}", align_bytes=64)
-            x_words.append(words)
             grouped = keep.tile([P, T * PACK], BF16, name=f"x_grouped{s}", align_bytes=64)
             for c in range(T // W):
-                raw = x_raw[s, c]
-                src = raw[:].rearrange("p j (c i) -> p c j i", i=4)
-                dst = grouped[:, c * W * PACK : (c + 1) * W * PACK].rearrange("p (c i j) -> p c j i", i=4, j=PACK)
+                cols = slice(c * W, (c + 1) * W)
+                src = x_raw[s, c][:].rearrange("p j (c i) -> p c j i", i=4)
+                dst = grouped[:, PACK * cols.start : PACK * cols.stop].rearrange("p (c i j) -> p c j i", i=4, j=PACK)
                 cut = X_SCALAR // 4
-                nc.scalar.copy(dst[:, :cut], src[:, :cut])
-                nc.vector.tensor_copy(out=dst[:, cut:], in_=src[:, cut:])
-                nc.vector.quantize_mx(
-                    out=words[:, c * W : (c + 1) * W].bitcast(FP8X4),
-                    scales=x_scales[4 * s : P, c * W : (c + 1) * W],
-                    in_=grouped[:, c * W * PACK : (c + 1) * W * PACK],
-                )
+                copy(True, dst[:, :cut], src[:, :cut])
+                copy(False, dst[:, cut:], src[:, cut:])
+                quantize(words, x_scales, grouped, cols, plane=4 * s)
             picked = keep.tile([P, S], U32, name=f"g_words{s}", align_bytes=64)
             nc.vector.tensor_copy(picked[:], words[:].indirect(offs_t[:]))
             g_words.append(picked)
         g_scales = keep.tile([P, S], U8, name="g_scales", align_bytes=64)
         nc.vector.tensor_copy(g_scales[:], x_scales[:].indirect(offs_t[:]))
 
-        h_codes, h_scales = [], []
-        HALF = S // 2
-        for h in range(HALVES):
-            if h == 0:
-                banks = {(t, 0): psum.tile([P, S], F32, name=f"bank{t}", tag=f"b{t}") for t in range(PACK)}
-                blocks = [slice(0, S)]
-            else:
-                banks = {
-                    (t, b): psum.tile([P, HALF], F32, name=f"bank1{t}{b}", tag=f"b{4 * (1 - b) + t}")
-                    for b in range(2)
-                    for t in range(PACK)
-                }
-                blocks = [slice(0, HALF), slice(HALF, S)]
+        def layer1(h, banks, blocks):
             for s in range(PASSES):
-                last = h == HALVES - 1 and s == PASSES - 1
-                grouped = keep.tile([P, W * PACK], BF16, name=f"w1_grouped{h}{s}", align_bytes=64)
-                m0 = 0
-                for raw in w1_raw[h, s]:
+                grouped, codes, scales = operand(f"w1_{h}{s}", W)
+                pieces = w1_raw[h, s]
+                m = P // len(pieces)
+                cut = W1_SCALAR[h][s] // len(pieces)
+                for c, raw in enumerate(pieces):
                     src = raw[:].rearrange("p j (m t) -> p m j t", t=PACK)
-                    m = P // len(w1_raw[h, s])
-                    dst = grouped[:].rearrange("p (t m j) -> p m j t", t=PACK, j=PACK)[:, m0 : m0 + m]
-                    m0 += m
-                    cut = (W1_SCALAR_LAST if last else W1_SCALAR[h]) * m // P
-                    nc.scalar.copy(dst[:, :cut], src[:, :cut])
-                    nc.vector.tensor_copy(out=dst[:, cut:], in_=src[:, cut:])
-                codes = keep.tile([P, W], U32, name=f"w1_codes{h}{s}", align_bytes=64)
-                scales = keep.tile([P, W], U8, name=f"w1_scales{h}{s}", align_bytes=64)
-                step = 2 * P if last else W
+                    dst = grouped[:].rearrange("p (t m j) -> p m j t", t=PACK, j=PACK)[:, c * m : (c + 1) * m]
+                    copy(True, dst[:, :cut], src[:, :cut])
+                    copy(False, dst[:, cut:], src[:, cut:])
+                step = W // len(pieces)
                 for q in range(0, W, step):
-                    nc.vector.quantize_mx(
-                        out=codes[:, q : q + step].bitcast(FP8X4),
-                        scales=scales[:, q : q + step],
-                        in_=grouped[:, PACK * q : PACK * (q + step)],
-                    )
+                    quantize(codes, scales, grouped, slice(q, q + step))
                 for b, cols in enumerate(blocks):
                     for t in range(PACK):
                         nc.tensor.matmul_mx(
-                            out=banks[t, b][:],
+                            out=banks[b][t][:],
                             lhsT=codes[:, t * P : (t + 1) * P].bitcast(FP8X4),
                             lhsT_scale=scales[:, t * P : (t + 1) * P],
                             rhs=g_words[s][:, cols].bitcast(FP8X4),
@@ -153,59 +142,67 @@ def tile_picked_sub_mlp_relu2_sub_e_kernel(tc, xT, w1, w2, gate, offs, pos1, pos
                             start=(s == 0),
                             stop=(s == PASSES - 1),
                         )
+
+        def relu(h, banks, blocks, on_scalar):
             r = keep.tile([P, PACK, S], F32, name=f"r{h}")
             for b, cols in enumerate(blocks):
                 for t in range(PACK):
-                    if t % 2 == 0:
-                        nc.scalar.activation(r[:, t, cols], banks[t, b][:], ACT.Relu)
+                    if on_scalar[b][t]:
+                        nc.scalar.activation(r[:, t, cols], banks[b][t][:], ACT.Relu)
                     else:
-                        nc.vector.tensor_scalar_max(r[:, t, cols], banks[t, b][:], 0.0)
-            h_grouped = keep.tile([P, S * PACK], BF16, name=f"h_grouped{h}", align_bytes=64)
-            codes = keep.tile([P, S], U32, name=f"h_codes{h}", align_bytes=64)
-            scales = keep.tile([P, S], U8, name=f"h_scales{h}", align_bytes=64)
-            for b in range(2):
-                src = r[:, :, b * HALF : (b + 1) * HALF].rearrange("p t (c i) -> p c t i", i=4)
-                dst = h_grouped[:, b * HALF * PACK : (b + 1) * HALF * PACK].rearrange("p (c i t) -> p c t i", i=4, t=PACK)
-                if b == 1:
-                    nc.scalar.activation(dst, src, ACT.Square)
-                else:
-                    nc.vector.tensor_tensor(dst, src, src, ALU.mult)
-            for b in range(2):
-                nc.vector.quantize_mx(
-                    out=codes[:, b * HALF : (b + 1) * HALF].bitcast(FP8X4),
-                    scales=scales[:, b * HALF : (b + 1) * HALF],
-                    in_=h_grouped[:, b * HALF * PACK : (b + 1) * HALF * PACK],
-                )
-            h_codes.append(codes)
-            h_scales.append(scales)
+                        nc.vector.tensor_scalar_max(r[:, t, cols], banks[b][t][:], 0.0)
+            return r
 
+        def square(h, r):
+            grouped, codes, scales = operand(f"h{h}", S)
+            for b in range(2):
+                for q in (2 * b, 2 * b + 1):
+                    src = r[:, :, q * P : (q + 1) * P].rearrange("p t (c i) -> p c t i", i=4)
+                    dst = grouped[:, q * P * PACK : (q + 1) * P * PACK].rearrange("p (c i t) -> p c t i", i=4, t=PACK)
+                    if SQUARE[h][q]:
+                        nc.scalar.activation(dst, src, ACT.Square)
+                    else:
+                        nc.vector.tensor_tensor(dst, src, src, ALU.mult)
+                quantize(codes, scales, grouped, slice(b * HALF, (b + 1) * HALF))
+            return codes, scales
+
+        whole = [slice(0, S)]
+        halves = [slice(0, HALF), slice(HALF, S)]
+        banks0 = [[psum.tile([P, S], F32, name=f"bank0{t}", tag=f"b{t}") for t in range(PACK)]]
+        layer1(0, banks0, whole)
+        r0 = relu(0, banks0, whole, [RELU0])
+        banks1 = [
+            [psum.tile([P, HALF], F32, name=f"bank1{b}{t}", tag=f"b{4 * (1 - b) + t}") for t in range(PACK)] for b in range(2)
+        ]
+        layer1(1, banks1, halves)
+        hidden0 = square(0, r0)
+        prepare_w2()
+        r1 = relu(1, banks1, halves, RELU1)
+        hidden1 = square(1, r1)
+
+        y = keep.tile([P, S], F32, name="y")
         y_banks = [psum.tile([P, HALF], F32, name=f"y_bank{b}", tag=f"b{4 + b}") for b in range(2)]
-        for b in range(2):
-            cols = slice(b * HALF, (b + 1) * HALF)
-            for h in range(HALVES):
+        for b, cols in enumerate(halves):
+            for h, (codes, scales) in enumerate((hidden0, hidden1)):
                 nc.tensor.matmul_mx(
                     out=y_banks[b][:],
-                    lhsT=w2_codes[:, h, :].bitcast(FP8X4),
-                    lhsT_scale=w2_scales[:, h, :],
-                    rhs=h_codes[h][:, cols].bitcast(FP8X4),
-                    rhs_scale=h_scales[h][:, cols],
+                    lhsT=w2_codes[:, h * N : (h + 1) * N].bitcast(FP8X4),
+                    lhsT_scale=w2_scales[:, h * N : (h + 1) * N],
+                    rhs=codes[:, cols].bitcast(FP8X4),
+                    rhs_scale=scales[:, cols],
                     start=(h == 0),
                     stop=(h == HALVES - 1),
                 )
+            copy(b == 0, y[:, cols], y_banks[b][:])
 
-        y = keep.tile([P, S], F32, name="y")
-        nc.scalar.copy(y[:, : S // 2], y_banks[0][:])
-        nc.vector.tensor_copy(out=y[:, S // 2 :], in_=y_banks[1][:])
-        prods = []
-        for d in range(D):
-            prod = keep.tile([P, V], F32, name=f"prod{d}")
-            nc.vector.tensor_tensor(prod[:], y[:].indirect(pos_t[d][:]), gate_t[:, d, :], ALU.mult)
-            prods.append(prod)
+        prods = [keep.tile([P, V], F32, name=f"prod{d}") for d in range(D)]
         pair = keep.tile([P, V], F32, name="pair")
         result = keep.tile([P, V], F32, name="result")
-        halves = [slice(0, V // 2), slice(V // 2, V)]
-        for cols in halves:
-            nc.vector.tensor_tensor(pair[:, cols], prods[0][:, cols], prods[1][:, cols], ALU.add)
-        for cols in halves:
-            nc.vector.tensor_tensor(result[:, cols], pair[:, cols], prods[2][:, cols], ALU.add)
-            (nc.sync if cols.start == 0 else nc.scalar).dma_start(out=out[:, cols], in_=result[:, cols])
+        for d in range(D):
+            nc.vector.tensor_tensor(prods[d][:], y[:].indirect(pos_t[d][:]), gate_t[:, d, :], ALU.mult)
+        parts = [slice(0, V // 2), slice(V // 2, V)]
+        for part in parts:
+            nc.vector.tensor_tensor(pair[:, part], prods[0][:, part], prods[1][:, part], ALU.add)
+        for part, queue in zip(parts, (nc.sync, nc.scalar)):
+            nc.vector.tensor_tensor(result[:, part], pair[:, part], prods[2][:, part], ALU.add)
+            queue.dma_start(out=out[:, part], in_=result[:, part])

@@ -22,11 +22,10 @@ HALVES = H // K_PASS
 W = 512
 HALF = S // 2
 
-X_SCALAR = 320
 W1_SCALAR = ((80, 80, 80), (32, 32, 48))
 RELU0 = (True, False, True, True)
-RELU1 = ((True, False, True, False), (True, False, True, True))
-SQUARE = ((True, True, True, False), (False, True, False, True))
+RELU1 = ((True, False, True, False), (True, True, True, False))
+SQUARE = ((True, False, True, True), (True, False, True, False))
 
 
 def tile_picked_sub_mlp_relu2_sub_e_kernel(tc, xT, w1, w2, gate, offs, pos1, pos2, pos3, out):
@@ -72,8 +71,7 @@ def tile_picked_sub_mlp_relu2_sub_e_kernel(tc, xT, w1, w2, gate, offs, pos1, pos
 
         x_raw, w1_raw = {}, {}
         for s in range(PASSES):
-            for c in range(T // W):
-                x_raw[s, c] = load_rows(f"x_raw{s}{c}", xT, s, c * W, W)
+            x_raw[s] = load_rows(f"x_raw{s}", xT, s, 0, T)
             if s == 0:
                 nc.sync.dma_start(offs_t[:], offs)
         for h in range(HALVES):
@@ -105,12 +103,11 @@ def tile_picked_sub_mlp_relu2_sub_e_kernel(tc, xT, w1, w2, gate, offs, pos1, pos
             grouped = keep.tile([P, T * PACK], BF16, name=f"x_grouped{s}", align_bytes=64)
             for c in range(T // W):
                 cols = slice(c * W, (c + 1) * W)
-                src = x_raw[s, c][:].rearrange("p j (c i) -> p c j i", i=4)
+                src = x_raw[s][:, :, cols].rearrange("p j (c i) -> p c j i", i=4)
                 dst = grouped[:, PACK * cols.start : PACK * cols.stop].rearrange("p (c i j) -> p c j i", i=4, j=PACK)
-                cut = X_SCALAR // 4
-                copy(True, dst[:, :cut], src[:, :cut])
-                copy(False, dst[:, cut:], src[:, cut:])
-                quantize(words, x_scales, grouped, cols, plane=4 * s)
+                copy(c == 0, dst, src)
+            for c in reversed(range(T // W)):
+                quantize(words, x_scales, grouped, slice(c * W, (c + 1) * W), plane=4 * s)
             picked = keep.tile([P, S], U32, name=f"g_words{s}", align_bytes=64)
             nc.vector.tensor_copy(picked[:], words[:].indirect(offs_t[:]))
             g_words.append(picked)

@@ -22,9 +22,9 @@ HALVES = H // K_PASS
 W = 512
 HALF = S // 2
 
-W1_SCALAR = ((80, 80, 80), (32, 32, 48))
+W1_SCALAR = ((112, 112, 112), (48, 48, 48))
 RELU0 = (True, False, True, True)
-RELU1 = ((True, False, True, False), (True, True, True, False))
+RELU1 = ((True, False, True, False), (True, False, True, True))
 SQUARE = ((True, False, True, True), (True, False, True, False))
 
 
@@ -76,7 +76,7 @@ def tile_picked_sub_mlp_relu2_sub_e_kernel(tc, xT, w1, w2, gate, offs, pos1, pos
                 nc.sync.dma_start(offs_t[:], offs)
         for h in range(HALVES):
             for s in range(PASSES):
-                pieces = 2 if h == 1 and s == PASSES - 1 else 1
+                pieces = 1
                 w1_raw[h, s] = [
                     load_rows(f"w1_raw{h}{s}{c}", w1, s, h * W + c * (W // pieces), W // pieces) for c in range(pieces)
                 ]
@@ -97,7 +97,13 @@ def tile_picked_sub_mlp_relu2_sub_e_kernel(tc, xT, w1, w2, gate, offs, pos1, pos
                 )
             quantize(w2_codes, w2_scales, w2_grouped, slice(0, HALVES * N))
 
-        g_words = []
+        x_words, g_words = [], []
+
+        def gather_words(s):
+            picked = keep.tile([P, S], U32, name=f"g_words{s}", align_bytes=64)
+            nc.vector.tensor_copy(picked[:], x_words[s][:].indirect(offs_t[:]))
+            g_words.append(picked)
+
         for s in range(PASSES):
             words = keep.tile([P, T], U32, name=f"x_words{s}", align_bytes=64)
             grouped = keep.tile([P, T * PACK], BF16, name=f"x_grouped{s}", align_bytes=64)
@@ -106,13 +112,16 @@ def tile_picked_sub_mlp_relu2_sub_e_kernel(tc, xT, w1, w2, gate, offs, pos1, pos
                 src = x_raw[s][:, :, cols].rearrange("p j (c i) -> p c j i", i=4)
                 dst = grouped[:, PACK * cols.start : PACK * cols.stop].rearrange("p (c i j) -> p c j i", i=4, j=PACK)
                 copy(c == 0, dst, src)
+            if s > 0:
+                gather_words(s - 1)
             for c in reversed(range(T // W)):
                 quantize(words, x_scales, grouped, slice(c * W, (c + 1) * W), plane=4 * s)
-            picked = keep.tile([P, S], U32, name=f"g_words{s}", align_bytes=64)
-            nc.vector.tensor_copy(picked[:], words[:].indirect(offs_t[:]))
-            g_words.append(picked)
+            x_words.append(words)
         g_scales = keep.tile([P, S], U8, name="g_scales", align_bytes=64)
-        nc.vector.tensor_copy(g_scales[:], x_scales[:].indirect(offs_t[:]))
+
+        def gather_last():
+            gather_words(PASSES - 1)
+            nc.vector.tensor_copy(g_scales[:], x_scales[:].indirect(offs_t[:]))
 
         def layer1(h, banks, blocks):
             for s in range(PASSES):
@@ -125,7 +134,9 @@ def tile_picked_sub_mlp_relu2_sub_e_kernel(tc, xT, w1, w2, gate, offs, pos1, pos
                     dst = grouped[:].rearrange("p (t m j) -> p m j t", t=PACK, j=PACK)[:, c * m : (c + 1) * m]
                     copy(True, dst[:, :cut], src[:, :cut])
                     copy(False, dst[:, cut:], src[:, cut:])
-                step = W // len(pieces)
+                if h == 0 and s == 0:
+                    gather_last()
+                step = W // 2 if h == 1 and s == PASSES - 1 else W
                 for q in range(0, W, step):
                     quantize(codes, scales, grouped, slice(q, q + step))
                 for b, cols in enumerate(blocks):
@@ -190,7 +201,7 @@ def tile_picked_sub_mlp_relu2_sub_e_kernel(tc, xT, w1, w2, gate, offs, pos1, pos
                     start=(h == 0),
                     stop=(h == HALVES - 1),
                 )
-            copy(b == 0, y[:, cols], y_banks[b][:])
+            nc.scalar.copy(y[:, cols], y_banks[b][:])
 
         prods = [keep.tile([P, V], F32, name=f"prod{d}") for d in range(D)]
         pair = keep.tile([P, V], F32, name="pair")

@@ -22,9 +22,9 @@ HALVES = H // K_PASS
 W = 512
 HALF = S // 2
 
-W1_SCALAR = ((112, 112, 112), (48, 48, 48))
+W1_SCALAR = ((112, 112, 112), (32, 32, 32))
 RELU0 = (True, False, True, True)
-RELU1 = ((True, False, True, False), (True, False, True, True))
+RELU1 = ((True, False, True, False), (True, False, True, False))
 SQUARE = ((True, False, True, True), (True, False, True, False))
 
 
@@ -80,12 +80,11 @@ def tile_picked_sub_mlp_relu2_sub_e_kernel(tc, xT, w1, w2, gate, offs, pos1, pos
                 w1_raw[h, s] = [
                     load_rows(f"w1_raw{h}{s}{c}", w1, s, h * W + c * (W // pieces), W // pieces) for c in range(pieces)
                 ]
-            if h == 0:
-                for d, pos in enumerate((pos1, pos2, pos3)):
-                    nc.sync.dma_start(pos_t[d][:], pos)
         load_w2()
         gate_t = keep.tile([P, D, V], F32, name="gate_t")
         nc.sync.dma_start(out=gate_t[:], in_=gate.rearrange("d m v -> m d v"))
+        for d, pos in enumerate((pos1, pos2, pos3)):
+            nc.sync.dma_start(pos_t[d][:], pos)
 
         w2_grouped, w2_codes, w2_scales = operand("w2", HALVES * N)
 

from contextlib import ExitStack

import concourse.mybir as mybir

K, T, S, H, N, D, V = 1536, 1024, 512, 1024, 128, 3, 256
FLOPS = 2 * S * (K * H + H * N)

F32 = mybir.dt.float32
BF16 = mybir.dt.bfloat16
U32 = mybir.dt.uint32
U16 = mybir.dt.uint16
U8 = mybir.dt.uint8
FP8X4 = mybir.dt.float8_e4m3fn_x4
ACT = mybir.ActivationFunctionType
ALU = mybir.AluOpType

P = 128
PACK = 4
K_PASS = P * PACK
PASSES = K // K_PASS
HALVES = H // K_PASS
W = 512
HALF = S // 2

W1_SCALAR = ((112, 112, 112), (32, 32, 32))
RELU0 = (True, False, True, True)
RELU1 = ((True, False, True, False), (True, False, True, False))
SQUARE = ((True, False, True, True), (True, False, True, False))


def tile_picked_sub_mlp_relu2_sub_e_kernel(tc, xT, w1, w2, gate, offs, pos1, pos2, pos3, out):
    nc = tc.nc
    with ExitStack() as ctx:
        keep = ctx.enter_context(tc.tile_pool(name="keep", bufs=1))
        psum = ctx.enter_context(tc.psum_pool(name="psum", bufs=1))

        def copy(on_scalar, dst, src):
            if on_scalar:
                nc.scalar.copy(dst, src)
            else:
                nc.vector.tensor_copy(out=dst, in_=src)

        def quantize(codes, scales, grouped, cols, plane=0):
            nc.vector.quantize_mx(
                out=codes[:, cols].bitcast(FP8X4),
                scales=scales[plane:P, cols],
                in_=grouped[:, PACK * cols.start : PACK * cols.stop],
            )

        def operand(name, width):
            return (
                keep.tile([P, width * PACK], BF16, name=f"{name}_grouped", align_bytes=64),
                keep.tile([P, width], U32, name=f"{name}_codes", align_bytes=64),
                keep.tile([P, width], U8, name=f"{name}_scales", align_bytes=64),
            )

        offs_t = keep.tile([P, S // 16], U16, name="offs_t")
        pos_t = [keep.tile([P, V // 16], U16, name=f"pos{d}_t") for d in range(D)]
        w2_raw = keep.tile([P, HALVES, PACK, N], F32, name="w2_raw")
        x_scales = keep.tile([P, T], U8, name="x_scales", align_bytes=64)
        nc.gpsimd.memset(x_scales[:], 0)

        def load_rows(name, source, s, first, width):
            raw = keep.tile([P, PACK, width], F32, name=name)
            rows = source[s * K_PASS : (s + 1) * K_PASS, first : first + width]
            nc.sync.dma_start(out=raw[:], in_=rows.rearrange("(p j) w -> p j w", j=PACK))
            return raw

        def load_w2():
            nc.sync.dma_start(out=w2_raw[:], in_=w2.rearrange("(g p j) m -> p g j m", p=P, j=PACK))

        x_raw, w1_raw = {}, {}
        for s in range(PASSES):
            x_raw[s] = load_rows(f"x_raw{s}", xT, s, 0, T)
            if s == 0:
                nc.sync.dma_start(offs_t[:], offs)
        for h in range(HALVES):
            for s in range(PASSES):
                pieces = 1
                w1_raw[h, s] = [
                    load_rows(f"w1_raw{h}{s}{c}", w1, s, h * W + c * (W // pieces), W // pieces) for c in range(pieces)
                ]
        load_w2()
        gate_t = keep.tile([P, D, V], F32, name="gate_t")
        nc.sync.dma_start(out=gate_t[:], in_=gate.rearrange("d m v -> m d v"))
        for d, pos in enumerate((pos1, pos2, pos3)):
            nc.sync.dma_start(pos_t[d][:], pos)

        w2_grouped, w2_codes, w2_scales = operand("w2", HALVES * N)

        def prepare_w2():
            for g in range(HALVES):
                nc.vector.tensor_copy(
                    out=w2_grouped[:, g * N * PACK : (g + 1) * N * PACK].rearrange("p (c i j) -> p c j i", i=4, j=PACK),
                    in_=w2_raw[:, g].rearrange("p j (c i) -> p c j i", i=4),
                )
            quantize(w2_codes, w2_scales, w2_grouped, slice(0, HALVES * N))

        x_words, g_words = [], []

        def gather_words(s):
            picked = keep.tile([P, S], U32, name=f"g_words{s}", align_bytes=64)
            nc.vector.tensor_copy(picked[:], x_words[s][:].indirect(offs_t[:]))
            g_words.append(picked)

        for s in range(PASSES):
            words = keep.tile([P, T], U32, name=f"x_words{s}", align_bytes=64)
            grouped = keep.tile([P, T * PACK], BF16, name=f"x_grouped{s}", align_bytes=64)
            for c in range(T // W):
                cols = slice(c * W, (c + 1) * W)
                src = x_raw[s][:, :, cols].rearrange("p j (c i) -> p c j i", i=4)
                dst = grouped[:, PACK * cols.start : PACK * cols.stop].rearrange("p (c i j) -> p c j i", i=4, j=PACK)
                copy(c == 0, dst, src)
            if s > 0:
                gather_words(s - 1)
            for c in reversed(range(T // W)):
                quantize(words, x_scales, grouped, slice(c * W, (c + 1) * W), plane=4 * s)
            x_words.append(words)
        g_scales = keep.tile([P, S], U8, name="g_scales", align_bytes=64)

        def gather_last():
            gather_words(PASSES - 1)
            nc.vector.tensor_copy(g_scales[:], x_scales[:].indirect(offs_t[:]))

        def layer1(h, banks, blocks):
            for s in range(PASSES):
                grouped, codes, scales = operand(f"w1_{h}{s}", W)
                pieces = w1_raw[h, s]
                m = P // len(pieces)
                cut = W1_SCALAR[h][s] // len(pieces)
                for c, raw in enumerate(pieces):
                    src = raw[:].rearrange("p j (m t) -> p m j t", t=PACK)
                    dst = grouped[:].rearrange("p (t m j) -> p m j t", t=PACK, j=PACK)[:, c * m : (c + 1) * m]
                    copy(True, dst[:, :cut], src[:, :cut])
                    copy(False, dst[:, cut:], src[:, cut:])
                if h == 0 and s == 0:
                    gather_last()
                step = W // 2 if h == 1 and s == PASSES - 1 else W
                for q in range(0, W, step):
                    quantize(codes, scales, grouped, slice(q, q + step))
                for b, cols in enumerate(blocks):
                    for t in range(PACK):
                        nc.tensor.matmul_mx(
                            out=banks[b][t][:],
                            lhsT=codes[:, t * P : (t + 1) * P].bitcast(FP8X4),
                            lhsT_scale=scales[:, t * P : (t + 1) * P],
                            rhs=g_words[s][:, cols].bitcast(FP8X4),
                            rhs_scale=g_scales[4 * s : P, cols],
                            start=(s == 0),
                            stop=(s == PASSES - 1),
                        )

        def relu(h, banks, blocks, on_scalar):
            r = keep.tile([P, PACK, S], F32, name=f"r{h}")
            for b, cols in enumerate(blocks):
                for t in range(PACK):
                    if on_scalar[b][t]:
                        nc.scalar.activation(r[:, t, cols], banks[b][t][:], ACT.Relu)
                    else:
                        nc.vector.tensor_scalar_max(r[:, t, cols], banks[b][t][:], 0.0)
            return r

        def square(h, r):
            grouped, codes, scales = operand(f"h{h}", S)
            for b in range(2):
                for q in (2 * b, 2 * b + 1):
                    src = r[:, :, q * P : (q + 1) * P].rearrange("p t (c i) -> p c t i", i=4)
                    dst = grouped[:, q * P * PACK : (q + 1) * P * PACK].rearrange("p (c i t) -> p c t i", i=4, t=PACK)
                    if SQUARE[h][q]:
                        nc.scalar.activation(dst, src, ACT.Square)
                    else:
                        nc.vector.tensor_tensor(dst, src, src, ALU.mult)
                quantize(codes, scales, grouped, slice(b * HALF, (b + 1) * HALF))
            return codes, scales

        whole = [slice(0, S)]
        halves = [slice(0, HALF), slice(HALF, S)]
        banks0 = [[psum.tile([P, S], F32, name=f"bank0{t}", tag=f"b{t}") for t in range(PACK)]]
        layer1(0, banks0, whole)
        r0 = relu(0, banks0, whole, [RELU0])
        banks1 = [
            [psum.tile([P, HALF], F32, name=f"bank1{b}{t}", tag=f"b{4 * (1 - b) + t}") for t in range(PACK)] for b in range(2)
        ]
        layer1(1, banks1, halves)
        hidden0 = square(0, r0)
        prepare_w2()
        r1 = relu(1, banks1, halves, RELU1)
        hidden1 = square(1, r1)

        y = keep.tile([P, S], F32, name="y")
        y_banks = [psum.tile([P, HALF], F32, name=f"y_bank{b}", tag=f"b{4 + b}") for b in range(2)]
        for b, cols in enumerate(halves):
            for h, (codes, scales) in enumerate((hidden0, hidden1)):
                nc.tensor.matmul_mx(
                    out=y_banks[b][:],
                    lhsT=w2_codes[:, h * N : (h + 1) * N].bitcast(FP8X4),
                    lhsT_scale=w2_scales[:, h * N : (h + 1) * N],
                    rhs=codes[:, cols].bitcast(FP8X4),
                    rhs_scale=scales[:, cols],
                    start=(h == 0),
                    stop=(h == HALVES - 1),
                )
            nc.scalar.copy(y[:, cols], y_banks[b][:])

        prods = [keep.tile([P, V], F32, name=f"prod{d}") for d in range(D)]
        pair = keep.tile([P, V], F32, name="pair")
        result = keep.tile([P, V], F32, name="result")
        for d in range(D):
            nc.vector.tensor_tensor(prods[d][:], y[:].indirect(pos_t[d][:]), gate_t[:, d, :], ALU.mult)
        parts = [slice(0, V // 2), slice(V // 2, V)]
        for part in parts:
            nc.vector.tensor_tensor(pair[:, part], prods[0][:, part], prods[1][:, part], ALU.add)
        for part, queue in zip(parts, (nc.sync, nc.scalar)):
            nc.vector.tensor_tensor(result[:, part], pair[:, part], prods[2][:, part], ALU.add)
            queue.dma_start(out=out[:, part], in_=result[:, part])
